import numpy as np
import ml_dtypes


def mxq(x, axis, fmt="e4m3"):
    dtype, down = {"e4m3": (ml_dtypes.float8_e4m3fn, 7), "e5m2": (ml_dtypes.float8_e5m2, 14)}[fmt]
    v = np.moveaxis(np.asarray(x, np.float32).astype(ml_dtypes.bfloat16).astype(np.float64), axis, -1)
    blocks = v.reshape(v.shape[:-1] + (-1, 32))
    amax = np.abs(blocks).max(-1, keepdims=True)
    byte = np.maximum(np.where(amax > 0, np.frexp(amax)[1] - 1 + 127, 0) - down, 1)
    scale = np.exp2(byte - 127.0)
    codes = (blocks / scale).astype(np.float32).astype(dtype).astype(np.float64)
    return np.moveaxis((codes * scale).reshape(v.shape), -1, axis)


WIDE = False


def mx_kscale(k):
    if not WIDE:
        return np.ones(k)
    levels = np.array([10, -10, 5, -5, 0])
    if k % 512:
        return np.exp2(np.random.permutation(np.resize(levels, k // 32))).repeat(32)
    a = np.empty((k // 512, 16))
    for p in range(k // 512):
        a[p, :8] = np.random.permutation(np.resize(levels, 8))
        for g in range(8):
            far = levels[np.abs(levels - a[p, g]) >= 10]
            a[p, g + 8] = far[np.random.randint(len(far))]
    return np.exp2(a.ravel()).repeat(32)


def f64(x):
    return np.asarray(x).astype(np.float64)


def striped(idx):
    return np.tile(idx.reshape(-1, 16).T, (8, 1)).astype(np.uint16)


def unstriped(offs):
    return offs[:16].T.reshape(-1).astype(np.int64)


E2M1 = np.array([0.0, 0.5, 1.0, 1.5, 2.0, 3.0, 4.0, 6.0, -0.0, -0.5, -1.0, -1.5, -2.0, -3.0, -4.0, -6.0])


def pack_weight(w, fmt):
    k, n = w.shape
    w = f64(np.asarray(w, np.float32).astype(ml_dtypes.bfloat16)).reshape(k // 32, 32, n)
    amax = np.abs(w).max(1)
    if fmt == "e4m3":
        byte = np.frexp(amax)[1] - 1 + 127 - 7
    else:
        mant, ex = np.frexp(amax / 6.0)
        byte = np.where(mant > 0.5, ex, ex - 1) + 127
    byte = np.clip(np.where(amax > 0, byte, 1), 1, 254)
    scaled = (w * np.exp2(127.0 - byte)[:, None, :]).reshape(k, n).astype(np.float32)
    by_word = np.ascontiguousarray(scaled.reshape(k // 512, 128, 4, n).transpose(0, 1, 3, 2))
    if fmt == "e4m3":
        words = by_word.astype(ml_dtypes.float8_e4m3fn).view(np.uint8)
    else:
        c = by_word.astype(ml_dtypes.float4_e2m1fn).view(np.uint8) & 0xF
        words = (c[..., 0::2] | (c[..., 1::2] << 4)).reshape(k // 512, 128, 2 * n)
    return np.ascontiguousarray(words), np.ascontiguousarray(byte.astype(np.uint8).reshape(k // 512, 16, n))


def unpack_weight(words, scales, fmt):
    g, _, n = scales.shape
    words = np.ascontiguousarray(words).reshape(g, 128, n, -1)
    if fmt == "e4m3":
        vals = words.view(ml_dtypes.float8_e4m3fn).astype(np.float64)
    else:
        nib = np.empty((g, 128, n, 4), np.uint8)
        nib[..., 0::2] = words & 0xF
        nib[..., 1::2] = words >> 4
        vals = E2M1[nib]
    vals = vals * np.repeat(np.exp2(scales.astype(np.float64) - 127.0), 8, axis=1)[..., None]
    return vals.transpose(0, 1, 3, 2).reshape(g * 512, n)


def gelu(v):
    return 0.5 * v * (1.0 + np.tanh(np.sqrt(2.0 / np.pi) * (v + 0.044715 * v**3)))


def twice(P):
    return np.random.permutation(np.repeat(np.arange(P), 2))


def bf(x):
    return np.asarray(x, np.float32).astype(ml_dtypes.bfloat16)


def planes(Y):
    n, m = Y.shape
    b = f64(bf(Y)).reshape(n // 32, 32, m)
    amax = np.abs(b).max(1)
    byte = np.clip(np.where(amax > 0, np.frexp(amax)[1] - 1 + 127 - 7, 1), 1, 254)
    codes = (b * np.exp2(127.0 - byte)[:, None, :]).reshape(n, m).astype(np.float32).astype(ml_dtypes.float8_e4m3fn).view(np.uint8)
    words = codes.reshape(n // 512, 128, 4, m).transpose(0, 1, 3, 2)
    return np.ascontiguousarray(words), np.ascontiguousarray(byte.astype(np.uint8).reshape(n // 512, 16, m))


K, H, T, S, P = 1024, 1024, 4096, 1024, 512

def setup_inputs():
    n = np.random.standard_normal
    s = mx_kscale(K)[:, None]
    u = mx_kscale(H)[:, None]
    d = {}
    d["tab_words"], d["tab_scales"] = pack_weight(n((K, T)) * s, "e4m3")
    d["offs"] = striped(np.random.permutation(T)[:S])
    d["pos1"] = striped(np.random.permutation(S)[:P])
    d["pos2"] = striped(np.random.permutation(S)[:P])
    d["pos3"] = striped(twice(P))
    d["w1"] = (1.5 * n((K, H)) / K**0.5 / s).astype(np.float32)
    d["w2_words"], d["w2_scales"] = pack_weight(0.6 * n((K, H)) / K**0.5 / s, "e2m1")
    d["gh"] = (np.exp(0.4 * n(H)) * u[:, 0]).astype(np.float32)
    d["gv"] = np.exp(0.3 * n(H)).astype(np.float32)
    d["w3"] = (0.7 * n((H, H)) / H**0.5 / u * np.exp(0.8 * n(H))[None, :]).astype(np.float32)
    return d

def reference(tab_words, tab_scales, offs, pos1, pos2, pos3, w1, w2_words, w2_scales, gh, gv, w3):
    v = unpack_weight(tab_words, tab_scales, "e4m3")[:, unstriped(offs)]
    w2 = unpack_weight(w2_words, w2_scales, "e2m1")
    bent = np.tanh(mxq(f64(w1), 0, "e4m3").T @ v)
    e = bent + (w2.T @ v)
    h = f64(gh)[:, None] * e
    z = f64(gv)[:, None] * h[:, unstriped(pos1)] - h[:, unstriped(pos2)]
    blk = mxq(f64(w3), 0, "e4m3").T @ mxq(z, 0, "e4m3")
    up = blk[:, unstriped(pos3)]
    y = up * e - up
    words, scales = planes(y)
    return y, words, scales

@@ -1,0 +1,345 @@
+from contextlib import ExitStack
+
+import concourse.mybir as mybir
+
+F32 = mybir.dt.float32
+BF16 = mybir.dt.bfloat16
+I32 = mybir.dt.int32
+U32 = mybir.dt.uint32
+U16 = mybir.dt.uint16
+U8 = mybir.dt.uint8
+FP8X4 = mybir.dt.float8_e4m3fn_x4
+FP4X4 = mybir.dt.float4_e2m1fn_x4
+ALU = mybir.AluOpType
+ACT = mybir.ActivationFunctionType
+
+K, H, T, S, NBLK = 1024, 1024, 4096, 1024, 512
+P = 128
+PACK = 4
+GROUP = P * PACK
+BANK = 512
+SPARE = 16
+KIB = 1024
+FLOPS = 2 * (2 * K * H * S + H * H * NBLK)
+
+
+def tile_list_stutter_block_encoder_kernel(
+    tc, tab_words, tab_scales, offs, pos1, pos2, pos3, w1, w2_words, w2_scales, gh, gv, w3, out_0, out_1, out_2
+):
+    nc = tc.nc
+    with ExitStack() as ctx:
+        lists = ctx.enter_context(tc.tile_pool(name="lists", bufs=1))
+        keep = ctx.enter_context(tc.tile_pool(name="keep", bufs=1))
+        ring = ctx.enter_context(tc.tile_pool(name="ring", bufs=1))
+        shared = ctx.enter_context(tc.tile_pool(name="shared", bufs=1))
+        psum = ctx.enter_context(tc.psum_pool(name="psum", bufs=4))
+
+        def load_list(src, name):
+            tile = lists.tile([P, src.shape[1]], U16, name=name)
+            nc.sync.dma_start(tile[:], src)
+            return tile
+
+        def load_table_pass(a):
+            tile = shared.tile([P, T], I32, name="tab%d" % a, offset=16 * a * KIB)
+            nc.sync.dma_start(tile[:], tab_words[a].rearrange("p t i -> p (t i)").bitcast(I32))
+            return tile
+
+        def load_weight_chunk(w, a, b, raw):
+            nc.sync.dma_start(
+                raw, w[a * GROUP : (a + 1) * GROUP, b * GROUP : (b + 1) * GROUP].rearrange("(p j) c -> p j c", j=PACK)
+            )
+
+        def load_gain(src, name, place):
+            tile = shared.tile([P, 2 * PACK], F32, name=name, offset=place * KIB)
+            nc.sync.dma_start(
+                tile[:].rearrange("p (b t) -> p b t", t=PACK), src.rearrange("(b p t) -> p b t", b=2, t=PACK)
+            )
+            return tile
+
+        def copy_on(engine, out, in_):
+            if engine == "scalar":
+                nc.scalar.copy(out, in_)
+            else:
+                nc.vector.tensor_copy(out, in_)
+
+        def bf_tile(name):
+            return ring.tile([P, PACK * BANK], BF16, name=name, tag="bf", bufs=3, align_bytes=64)
+
+        def round_weight(raw, name, engine="scalar"):
+            grouped = bf_tile(name)
+            dst = grouped[:].rearrange("p (t m j) -> p m j t", t=PACK, j=PACK)
+            src = raw.rearrange("p j (m t) -> p m j t", t=PACK)
+            for lo in (0, P // 2):
+                copy_on(engine, dst[:, lo : lo + P // 2], src[:, lo : lo + P // 2])
+            return grouped
+
+        def round_rows(rows, width, name, engine):
+            grouped = bf_tile(name)
+            dst = grouped[:, : PACK * width].rearrange("p (c i t) -> p c t i", i=PACK, t=PACK)
+            src = rows.rearrange("p t (c i) -> p c t i", i=PACK)
+            for lo in range(0, width // PACK, 64):
+                copy_on(engine, dst[:, lo : lo + 64], src[:, lo : lo + 64])
+            return grouped
+
+        def quantise(grouped, name):
+            codes = keep.tile([P, BANK], I32, name=name + "_c", align_bytes=64)
+            scales = keep.tile([P, BANK], U8, name=name + "_s", align_bytes=64)
+            nc.vector.quantize_mx(out=codes[:].bitcast(FP8X4), scales=scales[:], in_=grouped[:])
+            return codes, scales
+
+        tab_sc = shared.tile([P, T], U8, name="tab_sc", offset=54 * KIB)
+        nc.vector.memset(tab_sc[:, : T // 2].bitcast(I32), 0)
+        nc.gpsimd.memset(tab_sc[:, T // 2 :].bitcast(I32), 0)
+        w2_sc = keep.tile([P, 2 * H], U8, name="w2_sc", align_bytes=64)
+        nc.vector.memset(w2_sc[:].bitcast(I32), 0)
+        v_sc1 = keep.tile([P, S], U8, name="v_sc1", align_bytes=64)
+        nc.vector.memset(v_sc1[:].bitcast(I32), 0)
+        blk = [keep.tile([P, NBLK + SPARE], F32, name="blk%d" % s, align_bytes=64) for s in range(8)]
+        for s in range(8):
+            nc.vector.memset(blk[s][:, NBLK:], 0.0)
+
+        w1_raw = {}
+
+        def load_w1(a, b):
+            w1_raw[a, b] = shared.tile(
+                [P, PACK, BANK], F32, name="w1r%d%d" % (a, b), offset=(32 + 16 * b + 8 * a) * KIB
+            )
+            load_weight_chunk(w1, a, b, w1_raw[a, b][:])
+
+        offs_sb = load_list(offs, "offs_sb")
+        gv_sb = load_gain(gv, "gv_sb", 16)
+        gh_sb = load_gain(gh, "gh_sb", 40)
+        neg_gh = keep.tile([P, 2 * PACK], F32, name="neg_gh")
+        nc.scalar.activation(neg_gh[:], gh_sb[:], ACT.Copy, scale=-1.0)
+        gv_wide = [keep.tile([P, NBLK], F32, name="gv_wide%d" % s, align_bytes=64) for s in range(8)]
+        for s in range(8):
+            nc.scalar.copy(gv_wide[s][:], gv_sb[:, s : s + 1].to_broadcast([P, NBLK]))
+        tab0 = load_table_pass(0)
+        pos1_sb = load_list(pos1, "pos1_sb")
+        pos2_sb = load_list(pos2, "pos2_sb")
+        pos3_sb = load_list(pos3, "pos3_sb")
+        load_w1(0, 0)
+        for q in range(4):
+            nc.sync.dma_start(
+                tab_sc[32 * q : 32 * q + 8, :].bitcast(I32), tab_scales[:, 4 * q : 4 * q + 4, :].bitcast(I32)
+            )
+        w2_raw = ring.tile([P, 4 * H], U8, name="w2_raw", tag="zf1", bufs=1, align_bytes=64)
+        nc.sync.dma_start(
+            w2_raw[:].bitcast(I32).rearrange("p (a c) -> p a c", a=2),
+            w2_words.bitcast(I32).rearrange("a p c -> p a c"),
+        )
+        load_w1(1, 0)
+        for q in range(4):
+            nc.sync.dma_start(
+                w2_sc[32 * q : 32 * q + 4, :].bitcast(I32).rearrange("p (a c) -> p a c", a=2),
+                w2_scales[:, 4 * q : 4 * q + 4, :].bitcast(I32).rearrange("a r c -> r a c"),
+            )
+        tab1 = load_table_pass(1)
+
+        v_w = [keep.tile([P, S], U32, name="v_w%d" % a, align_bytes=64) for a in range(2)]
+        v_sc0 = keep.tile([P, S], U8, name="v_sc0", align_bytes=64)
+        nc.vector.tensor_copy(v_w[0][:], tab0[:].bitcast(U32).indirect(offs_sb[:]))
+        nc.vector.tensor_copy(v_sc0[:], tab_sc[:].indirect(offs_sb[:]))
+        nc.sync.dma_start(v_sc1[0:100, :].bitcast(I32), v_sc0[4:104, :].bitcast(I32))
+        v_sc = [v_sc0, v_sc1]
+        load_w1(0, 1)
+        load_w1(1, 1)
+
+        w2_c, w2_s = {}, {}
+
+        def deal_w2(b):
+            w2_c[b] = keep.tile([P, 2 * H], U8, name="w2_c%d" % b, align_bytes=64)
+            w2_s[b] = keep.tile([P, H], U8, name="w2_s%d" % b, align_bytes=64)
+            nc.vector.tensor_copy(
+                w2_c[b][:].bitcast(U16).rearrange("p (a t m) -> p a t m", a=2, t=PACK),
+                w2_raw[:].bitcast(U16).rearrange("p (a b m t) -> p b a t m", a=2, b=2, t=PACK)[:, b],
+            )
+            nc.vector.tensor_copy(
+                w2_s[b][:].rearrange("p (a t m) -> p a t m", a=2, t=PACK),
+                w2_sc[:].rearrange("p (a b m t) -> p b a t m", a=2, b=2, t=PACK)[:, b],
+            )
+
+        deal_w2(0)
+        w1_q, w3_q = {}, {}
+
+        def prep_w1(a, b):
+            w1_q[a, b] = quantise(round_weight(w1_raw[a, b][:], "w1g%d%d" % (a, b)), "w1q%d%d" % (a, b))
+
+        prep_w1(0, 0)
+        deal_w2(1)
+        prep_w1(1, 0)
+        for h in range(2):
+            nc.vector.tensor_copy(
+                v_w[1][:, h * BANK : (h + 1) * BANK],
+                tab1[:].bitcast(U32).indirect(offs_sb[:, h * 32 : (h + 1) * 32]),
+            )
+
+        w3_raw = {}
+        for b in range(2):
+            for a in range(2):
+                w3_raw[a, b] = shared.tile(
+                    [P, PACK, BANK], F32, name="w3r%d%d" % (a, b), offset=(32 - 16 * b + 8 * a) * KIB
+                )
+                load_weight_chunk(w3, a, b, w3_raw[a, b][:])
+
+        def prep_w3(a, b):
+            w3_q[a, b] = quantise(round_weight(w3_raw[a, b][:], "w3g%d%d" % (a, b)), "w3q%d%d" % (a, b))
+
+        e = [keep.tile([P, S], F32, name="e%d" % s, align_bytes=64) for s in range(8)]
+        zf = [ring.tile([P, PACK, NBLK], F32, name="zf%d" % b, tag="zf%d" % b, bufs=1, align_bytes=64) for b in range(2)]
+        z_q = {}
+
+        bent = {}
+
+        def bend(s, halves=(0, 1)):
+            b, t = divmod(s, PACK)
+            cols = slice(t * P, (t + 1) * P)
+            for h in halves:
+                js = slice(h * BANK, (h + 1) * BANK)
+                bent_in = psum.tile([P, BANK], F32, name="bent_in", tag="pa")
+                for a in range(2):
+                    codes, scales = w1_q[a, b]
+                    nc.tensor.matmul_mx(
+                        out=bent_in[:],
+                        lhsT=codes[:, cols].bitcast(FP8X4),
+                        lhsT_scale=scales[:, cols],
+                        rhs=v_w[a][:, js].bitcast(FP8X4),
+                        rhs_scale=v_sc[a][:, js],
+                        start=(a == 0),
+                        stop=(a == 1),
+                    )
+                bent[s, h] = ring.tile([P, BANK], F32, name="bent", tag="bent", bufs=4, align_bytes=64)
+                nc.scalar.activation(bent[s, h][:], bent_in[:], ACT.Tanh)
+
+        def features(s, h):
+            b, t = divmod(s, PACK)
+            js = slice(h * BANK, (h + 1) * BANK)
+            linear = psum.tile([P, BANK], F32, name="linear", tag="pb")
+            for a in range(2):
+                c0 = a * GROUP + t * P
+                nc.tensor.matmul_mx(
+                    out=linear[:],
+                    lhsT=w2_c[b][:, 2 * c0 : 2 * (c0 + P)].bitcast(FP4X4),
+                    lhsT_scale=w2_s[b][:, c0 : c0 + P],
+                    rhs=v_w[a][:, js].bitcast(FP8X4),
+                    rhs_scale=v_sc[a][:, js],
+                    start=(a == 0),
+                    stop=(a == 1),
+                )
+            nc.vector.tensor_tensor(e[s][:, js], linear[:], bent[s, h][:], ALU.add)
+
+        first = {}
+
+        def first_member(s):
+            first[s] = ring.tile([P, NBLK], F32, name="first", tag="first", bufs=2, align_bytes=64)
+            nc.vector.tensor_tensor(first[s][:], e[s][:].indirect(pos1_sb[:]), gv_wide[s][:], ALU.mult)
+
+        def second_member(s):
+            b, t = divmod(s, PACK)
+            nc.vector.tensor_tensor(zf[b][:, t, :], e[s][:].indirect(pos2_sb[:]), first[s][:], ALU.subtract)
+
+        def gain(s):
+            b, t = divmod(s, PACK)
+            if s == 7:
+                nc.vector.tensor_scalar(zf[b][:, t, :], zf[b][:, t, :], neg_gh[:, s : s + 1], None, ALU.mult)
+            else:
+                nc.scalar.activation(zf[b][:, t, :], zf[b][:, t, :], ACT.Copy, scale=neg_gh[:, s : s + 1])
+
+        em = {}
+
+        def minus_one(s):
+            nc.scalar.activation(e[s][:], e[s][:], ACT.Copy, bias=-1.0)
+            em[s] = e[s][:]
+
+        for h in range(2):
+            bend(0, (h,))
+            features(0, h)
+        bend(1)
+        for s in range(8):
+            if s + 2 < 8:
+                bend(s + 2)
+            if s + 1 < 8:
+                features(s + 1, 0)
+            first_member(s)
+            if s + 1 < 8:
+                features(s + 1, 1)
+            second_member(s)
+            if s < 2:
+                prep_w1(s, 1)
+            if s > 0:
+                gain(s - 1)
+            if s == 4:
+                z_q[0] = quantise(round_rows(zf[0][:], NBLK, "zg0", "scalar"), "zq0")
+            if s in (3, 5):
+                prep_w3((s - 3) // 2, 0)
+            if s in (2, 3, 6, 7):
+                minus_one((2, 3, 6, 7).index(s))
+        gain(7)
+        zg1 = round_rows(zf[1][:], NBLK, "zg1", "vector")
+        z_q[1] = quantise(zg1, "zq1")
+        late = ring.tile([P, PACK, S], F32, name="late", tag="zf1", bufs=1, align_bytes=64)
+        for t in range(PACK):
+            nc.vector.tensor_scalar(late[:, t, :], e[PACK + t][:], -1.0, None, ALU.add)
+            em[PACK + t] = late[:, t, :]
+
+        def block_results(s):
+            b, t = divmod(s, PACK)
+            cols = slice(t * P, (t + 1) * P)
+            acc = psum.tile([P, BANK], F32, name="acc", tag="pa")
+            for a in range(2):
+                codes, scales = w3_q[a, b]
+                nc.tensor.matmul_mx(
+                    out=acc[:],
+                    lhsT=codes[:, cols].bitcast(FP8X4),
+                    lhsT_scale=scales[:, cols],
+                    rhs=z_q[a][0][:].bitcast(FP8X4),
+                    rhs_scale=z_q[a][1][:],
+                    start=(a == 0),
+                    stop=(a == 1),
+                )
+            nc.scalar.copy(blk[s][:, :NBLK], acc[:])
+
+        y_c = [keep.tile([P, S], I32, name="y_c%d" % g, align_bytes=64) for g in range(2)]
+        y_s = [keep.tile([P, S], U8, name="y_s%d" % g, align_bytes=64) for g in range(2)]
+
+        def way_up(g, c0, width, engine, place):
+            cols = slice(c0, c0 + width)
+            last = engine == "vector"
+            y = shared.tile([P, PACK, width], F32, name="y%d_%d" % (g, c0), offset=place * KIB)
+            rows = out_0[g * GROUP : (g + 1) * GROUP, cols].rearrange("(p t) c -> p t c", t=PACK)
+            for t in range(PACK):
+                s = g * PACK + t
+                nc.vector.tensor_tensor(
+                    y[:, t, :], blk[s][:].indirect(pos3_sb[:, c0 // 16 : (c0 + width) // 16]), em[s][:, cols], ALU.mult
+                )
+                if last:
+                    nc.sync.dma_start(rows[:, t, :], y[:, t, :])
+            if not last:
+                nc.sync.dma_start(rows, y[:])
+            grouped = round_rows(y[:], width, "yg", engine)
+            nc.vector.quantize_mx(
+                out=y_c[g][:, cols].bitcast(FP8X4), scales=y_s[g][:, cols], in_=grouped[:, : PACK * width]
+            )
+            queue = nc.scalar if last else nc.sync
+            queue.dma_start(out_1[g, :, cols, :].rearrange("p m t -> p (m t)").bitcast(I32), y_c[g][:, cols])
+
+        def store_scales(g):
+            for q in range(4):
+                queue = nc.scalar if g == 1 and q == 3 else nc.sync
+                queue.dma_start(
+                    out_2[g, 4 * q : 4 * q + 4, :].bitcast(I32), y_s[g][32 * q : 32 * q + 4, :].bitcast(I32)
+                )
+
+        for s in range(4):
+            block_results(s)
+        prep_w3(0, 1)
+        prep_w3(1, 1)
+        way_up(0, 0, 512, "scalar", 0)
+        for s in range(4, 8):
+            block_results(s)
+        way_up(0, 512, 512, "scalar", 8)
+        store_scales(0)
+        way_up(1, 0, 512, "scalar", 48)
+        way_up(1, 512, 256, "scalar", 56)
+        way_up(1, 768, 256, "vector", 60)
+        store_scales(1)

@@ -51,7 +51,7 @@ def tile_list_stutter_block_encoder_kernel(
 
         def load_gain(src, name, place):
             tile = shared.tile([P, 2 * PACK], F32, name=name, offset=place * KIB)
-            nc.sync.dma_start(
+            nc.scalar.dma_start(
                 tile[:].rearrange("p (b t) -> p b t", t=PACK), src.rearrange("(b p t) -> p b t", b=2, t=PACK)
             )
             return tile
@@ -106,21 +106,21 @@ def tile_list_stutter_block_encoder_kernel(
             )
             load_weight_chunk(w1, a, b, w1_raw[a, b][:])
 
-        offs_sb = load_list(offs, "offs_sb")
-        gv_sb = load_gain(gv, "gv_sb", 16)
         gh_sb = load_gain(gh, "gh_sb", 40)
+        gv_sb = load_gain(gv, "gv_sb", 16)
         neg_gh = keep.tile([P, 2 * PACK], F32, name="neg_gh")
         nc.scalar.activation(neg_gh[:], gh_sb[:], ACT.Copy, scale=-1.0)
         gv_wide = [keep.tile([P, NBLK], F32, name="gv_wide%d" % s, align_bytes=64) for s in range(8)]
         for s in range(8):
             nc.scalar.copy(gv_wide[s][:], gv_sb[:, s : s + 1].to_broadcast([P, NBLK]))
         tab0 = load_table_pass(0)
+        offs_sb = load_list(offs, "offs_sb")
         pos1_sb = load_list(pos1, "pos1_sb")
         pos2_sb = load_list(pos2, "pos2_sb")
         pos3_sb = load_list(pos3, "pos3_sb")
         load_w1(0, 0)
         for q in range(4):
-            nc.sync.dma_start(
+            nc.gpsimd.dma_start(
                 tab_sc[32 * q : 32 * q + 8, :].bitcast(I32), tab_scales[:, 4 * q : 4 * q + 4, :].bitcast(I32)
             )
         w2_raw = ring.tile([P, 4 * H], U8, name="w2_raw", tag="zf1", bufs=1, align_bytes=64)
@@ -128,19 +128,19 @@ def tile_list_stutter_block_encoder_kernel(
             w2_raw[:].bitcast(I32).rearrange("p (a c) -> p a c", a=2),
             w2_words.bitcast(I32).rearrange("a p c -> p a c"),
         )
-        load_w1(1, 0)
         for q in range(4):
             nc.sync.dma_start(
                 w2_sc[32 * q : 32 * q + 4, :].bitcast(I32).rearrange("p (a c) -> p a c", a=2),
                 w2_scales[:, 4 * q : 4 * q + 4, :].bitcast(I32).rearrange("a r c -> r a c"),
             )
+        load_w1(1, 0)
         tab1 = load_table_pass(1)
 
         v_w = [keep.tile([P, S], U32, name="v_w%d" % a, align_bytes=64) for a in range(2)]
         v_sc0 = keep.tile([P, S], U8, name="v_sc0", align_bytes=64)
         nc.vector.tensor_copy(v_w[0][:], tab0[:].bitcast(U32).indirect(offs_sb[:]))
         nc.vector.tensor_copy(v_sc0[:], tab_sc[:].indirect(offs_sb[:]))
-        nc.sync.dma_start(v_sc1[0:100, :].bitcast(I32), v_sc0[4:104, :].bitcast(I32))
+        nc.sync.dma_start(v_sc1[0:112, :].bitcast(I32), v_sc0[4:116, :].bitcast(I32))
         v_sc = [v_sc0, v_sc1]
         load_w1(0, 1)
         load_w1(1, 1)
@@ -208,7 +208,7 @@ def tile_list_stutter_block_encoder_kernel(
                         start=(a == 0),
                         stop=(a == 1),
                     )
-                bent[s, h] = ring.tile([P, BANK], F32, name="bent", tag="bent", bufs=4, align_bytes=64)
+                bent[s, h] = ring.tile([P, BANK], F32, name="bent", tag="bent", bufs=8, align_bytes=64)
                 nc.scalar.activation(bent[s, h][:], bent_in[:], ACT.Tanh)
 
         def features(s, h):
@@ -228,22 +228,27 @@ def tile_list_stutter_block_encoder_kernel(
                 )
             nc.vector.tensor_tensor(e[s][:, js], linear[:], bent[s, h][:], ALU.add)
 
-        first = {}
+        first, second = {}, {}
+
+        def spent(s, h, name):
+            if s < 8:
+                return bent[s, h]
+            return ring.tile([P, BANK], F32, name=name, tag="bent", bufs=8, align_bytes=64)
 
         def first_member(s):
-            first[s] = ring.tile([P, NBLK], F32, name="first", tag="first", bufs=2, align_bytes=64)
+            first[s] = spent(s + 1, 1, "first")
             nc.vector.tensor_tensor(first[s][:], e[s][:].indirect(pos1_sb[:]), gv_wide[s][:], ALU.mult)
 
         def second_member(s):
-            b, t = divmod(s, PACK)
-            nc.vector.tensor_tensor(zf[b][:, t, :], e[s][:].indirect(pos2_sb[:]), first[s][:], ALU.subtract)
+            second[s] = spent(s + 2, 0, "second")
+            nc.vector.tensor_tensor(second[s][:], e[s][:].indirect(pos2_sb[:]), first[s][:], ALU.subtract)
 
         def gain(s):
             b, t = divmod(s, PACK)
             if s == 7:
-                nc.vector.tensor_scalar(zf[b][:, t, :], zf[b][:, t, :], neg_gh[:, s : s + 1], None, ALU.mult)
+                nc.vector.tensor_scalar(zf[b][:, t, :], second[s][:], neg_gh[:, s : s + 1], None, ALU.mult)
             else:
-                nc.scalar.activation(zf[b][:, t, :], zf[b][:, t, :], ACT.Copy, scale=neg_gh[:, s : s + 1])
+                nc.scalar.activation(zf[b][:, t, :], second[s][:], ACT.Copy, scale=neg_gh[:, s : s + 1])
 
         em = {}
 
@@ -255,15 +260,14 @@ def tile_list_stutter_block_encoder_kernel(
             bend(0, (h,))
             features(0, h)
         bend(1)
-        for s in range(8):
+        for s in range(7):
             if s + 2 < 8:
                 bend(s + 2)
-            if s + 1 < 8:
-                features(s + 1, 0)
+            features(s + 1, 0)
+            if s > 0:
+                second_member(s - 1)
+            features(s + 1, 1)
             first_member(s)
-            if s + 1 < 8:
-                features(s + 1, 1)
-            second_member(s)
             if s < 2:
                 prep_w1(s, 1)
             if s > 0:
@@ -272,8 +276,12 @@ def tile_list_stutter_block_encoder_kernel(
                 z_q[0] = quantise(round_rows(zf[0][:], NBLK, "zg0", "scalar"), "zq0")
             if s in (3, 5):
                 prep_w3((s - 3) // 2, 0)
-            if s in (2, 3, 6, 7):
-                minus_one((2, 3, 6, 7).index(s))
+            if s == 6:
+                prep_w3(0, 1)
+        first_member(7)
+        second_member(6)
+        gain(6)
+        second_member(7)
         gain(7)
         zg1 = round_rows(zf[1][:], NBLK, "zg1", "vector")
         z_q[1] = quantise(zg1, "zq1")
@@ -312,10 +320,7 @@ def tile_list_stutter_block_encoder_kernel(
                 nc.vector.tensor_tensor(
                     y[:, t, :], blk[s][:].indirect(pos3_sb[:, c0 // 16 : (c0 + width) // 16]), em[s][:, cols], ALU.mult
                 )
-                if last:
-                    nc.sync.dma_start(rows[:, t, :], y[:, t, :])
-            if not last:
-                nc.sync.dma_start(rows, y[:])
+            nc.sync.dma_start(rows, y[:])
             grouped = round_rows(y[:], width, "yg", engine)
             nc.vector.quantize_mx(
                 out=y_c[g][:, cols].bitcast(FP8X4), scales=y_s[g][:, cols], in_=grouped[:, : PACK * width]
@@ -325,18 +330,18 @@ def tile_list_stutter_block_encoder_kernel(
 
         def store_scales(g):
             for q in range(4):
-                queue = nc.scalar if g == 1 and q == 3 else nc.sync
+                queue = nc.scalar if g == 1 and q >= 2 else nc.sync
                 queue.dma_start(
                     out_2[g, 4 * q : 4 * q + 4, :].bitcast(I32), y_s[g][32 * q : 32 * q + 4, :].bitcast(I32)
                 )
 
         for s in range(4):
+            minus_one(s)
             block_results(s)
-        prep_w3(0, 1)
         prep_w3(1, 1)
-        way_up(0, 0, 512, "scalar", 0)
         for s in range(4, 8):
             block_results(s)
+        way_up(0, 0, 512, "scalar", 0)
         way_up(0, 512, 512, "scalar", 8)
         store_scales(0)
         way_up(1, 0, 512, "scalar", 48)

@@ -247,6 +247,10 @@ def tile_list_stutter_block_encoder_kernel(
             b, t = divmod(s, PACK)
             if s == 7:
                 nc.vector.tensor_scalar(zf[b][:, t, :], second[s][:], neg_gh[:, s : s + 1], None, ALU.mult)
+            elif s < 6:
+                nc.gpsimd.tensor_scalar(
+                    zf[b][:, t, :], second[s][:], neg_gh[:, s : s + 1], 0.0, ALU.mult, ALU.add
+                )
             else:
                 nc.scalar.activation(zf[b][:, t, :], second[s][:], ACT.Copy, scale=neg_gh[:, s : s + 1])
 
@@ -264,9 +268,9 @@ def tile_list_stutter_block_encoder_kernel(
             if s + 2 < 8:
                 bend(s + 2)
             features(s + 1, 0)
+            features(s + 1, 1)
             if s > 0:
                 second_member(s - 1)
-            features(s + 1, 1)
             first_member(s)
             if s < 2:
                 prep_w1(s, 1)

@@ -63,14 +63,14 @@ def tile_list_stutter_block_encoder_kernel(
                 nc.vector.tensor_copy(out, in_)
 
         def bf_tile(name):
-            return ring.tile([P, PACK * BANK], BF16, name=name, tag="bf", bufs=3, align_bytes=64)
+            return ring.tile([P, PACK * BANK], BF16, name=name, tag="bf", bufs=4, align_bytes=64)
 
-        def round_weight(raw, name, engine="scalar"):
+        def round_weight(raw, name, shares=(("scalar", 0, 64), ("scalar", 64, 128))):
             grouped = bf_tile(name)
             dst = grouped[:].rearrange("p (t m j) -> p m j t", t=PACK, j=PACK)
             src = raw.rearrange("p j (m t) -> p m j t", t=PACK)
-            for lo in (0, P // 2):
-                copy_on(engine, dst[:, lo : lo + P // 2], src[:, lo : lo + P // 2])
+            for engine, lo, hi in shares:
+                copy_on(engine, dst[:, lo:hi], src[:, lo:hi])
             return grouped
 
         def round_rows(rows, width, name, engine):
@@ -178,7 +178,7 @@ def tile_list_stutter_block_encoder_kernel(
         for b in range(2):
             for a in range(2):
                 w3_raw[a, b] = shared.tile(
-                    [P, PACK, BANK], F32, name="w3r%d%d" % (a, b), offset=(32 - 16 * b + 8 * a) * KIB
+                    [P, PACK, BANK], F32, name="w3r%d%d" % (a, b), offset=(16 + 24 * b + 8 * a) * KIB
                 )
                 load_weight_chunk(w3, a, b, w3_raw[a, b][:])
 
@@ -264,6 +264,7 @@ def tile_list_stutter_block_encoder_kernel(
             bend(0, (h,))
             features(0, h)
         bend(1)
+        w3_late = []
         for s in range(7):
             if s + 2 < 8:
                 bend(s + 2)
@@ -272,27 +273,56 @@ def tile_list_stutter_block_encoder_kernel(
             if s > 0:
                 second_member(s - 1)
             first_member(s)
-            if s < 2:
-                prep_w1(s, 1)
             if s > 0:
                 gain(s - 1)
+            if s < 2:
+                prep_w1(s, 1)
+            elif s < 4:
+                prep_w3(s - 2, 0)
+            elif s < 6:
+                w3_late.append(round_weight(w3_raw[s - 4, 1][:], "w3g%d1" % (s - 4)))
             if s == 4:
-                z_q[0] = quantise(round_rows(zf[0][:], NBLK, "zg0", "scalar"), "zq0")
-            if s in (3, 5):
-                prep_w3((s - 3) // 2, 0)
+                minus_one(0)
+            if s == 5:
+                zg0 = round_rows(zf[0][:], NBLK, "zg0", "scalar")
+                z_q[0] = quantise(zg0, "zq0")
+                minus_one(1)
             if s == 6:
-                prep_w3(0, 1)
-        first_member(7)
+                for r in range(2, 6):
+                    minus_one(r)
+        first[7] = zg0[:].bitcast(F32)[:, :NBLK]
+        nc.vector.tensor_tensor(first[7], e[7][:].indirect(pos1_sb[:]), gv_wide[7][:], ALU.mult)
         second_member(6)
         gain(6)
-        second_member(7)
-        gain(7)
-        zg1 = round_rows(zf[1][:], NBLK, "zg1", "vector")
-        z_q[1] = quantise(zg1, "zq1")
-        late = ring.tile([P, PACK, S], F32, name="late", tag="zf1", bufs=1, align_bytes=64)
-        for t in range(PACK):
-            nc.vector.tensor_scalar(late[:, t, :], e[PACK + t][:], -1.0, None, ALU.add)
-            em[PACK + t] = late[:, t, :]
+        last = spent(9, 0, "second")
+        zg1 = bf_tile("zg1")
+        z_q[1] = (
+            keep.tile([P, BANK], I32, name="zq1_c", align_bytes=64),
+            keep.tile([P, BANK], U8, name="zq1_s", align_bytes=64),
+        )
+        halves = [slice(0, 256), slice(256, 512)]
+        for h in range(2):
+            nc.vector.tensor_tensor(
+                last[:, halves[h]], e[7][:].indirect(pos2_sb[:, 16 * h : 16 * h + 16]), first[7][:, halves[h]],
+                ALU.subtract,
+            )
+        dst = zg1[:].rearrange("p (c i t) -> p c t i", i=PACK, t=PACK)
+        src = zf[1][:].rearrange("p t (c i) -> p c t i", i=PACK)
+        nc.scalar.activation(zf[1][:, 3, halves[0]], last[:, halves[0]], ACT.Copy, scale=neg_gh[:, 7:8])
+        nc.scalar.copy(dst[:, :64], src[:, :64])
+        nc.vector.tensor_scalar(zf[1][:, 3, halves[1]], last[:, halves[1]], neg_gh[:, 7:8], None, ALU.mult)
+        nc.vector.tensor_copy(dst[:, 64:], src[:, 64:])
+        for h in (1, 0):
+            nc.vector.quantize_mx(
+                out=z_q[1][0][:, halves[h]].bitcast(FP8X4),
+                scales=z_q[1][1][:, halves[h]],
+                in_=zg1[:, 1024 * h : 1024 * h + 1024],
+            )
+        late = ring.tile([P, 2, BANK], I32, name="late", tag="zf1", bufs=1, align_bytes=64)
+        for a in range(2):
+            scales = keep.tile([P, BANK], U8, name="w3q%d1_s" % a, align_bytes=64)
+            nc.vector.quantize_mx(out=late[:, a, :].bitcast(FP8X4), scales=scales[:], in_=w3_late[a][:])
+            w3_q[a, 1] = (late[:, a, :], scales)
 
         def block_results(s):
             b, t = divmod(s, PACK)
@@ -312,11 +342,10 @@ def tile_list_stutter_block_encoder_kernel(
             nc.scalar.copy(blk[s][:, :NBLK], acc[:])
 
         y_c = [keep.tile([P, S], I32, name="y_c%d" % g, align_bytes=64) for g in range(2)]
-        y_s = [keep.tile([P, S], U8, name="y_s%d" % g, align_bytes=64) for g in range(2)]
+        y_s = keep.tile([P, S], U8, name="y_s", align_bytes=64)
 
         def way_up(g, c0, width, engine, place):
             cols = slice(c0, c0 + width)
-            last = engine == "vector"
             y = shared.tile([P, PACK, width], F32, name="y%d_%d" % (g, c0), offset=place * KIB)
             rows = out_0[g * GROUP : (g + 1) * GROUP, cols].rearrange("(p t) c -> p t c", t=PACK)
             for t in range(PACK):
@@ -324,31 +353,33 @@ def tile_list_stutter_block_encoder_kernel(
                 nc.vector.tensor_tensor(
                     y[:, t, :], blk[s][:].indirect(pos3_sb[:, c0 // 16 : (c0 + width) // 16]), em[s][:, cols], ALU.mult
                 )
-            nc.sync.dma_start(rows, y[:])
+            queue = nc.scalar if engine == "vector" else nc.sync
+            queue.dma_start(rows, y[:])
             grouped = round_rows(y[:], width, "yg", engine)
             nc.vector.quantize_mx(
-                out=y_c[g][:, cols].bitcast(FP8X4), scales=y_s[g][:, cols], in_=grouped[:, : PACK * width]
+                out=y_c[g][:, cols].bitcast(FP8X4), scales=y_s[4 * g :, cols], in_=grouped[:, : PACK * width]
             )
-            queue = nc.scalar if last else nc.sync
+
+        def store_words(g, c0, width, queue):
+            cols = slice(c0, c0 + width)
             queue.dma_start(out_1[g, :, cols, :].rearrange("p m t -> p (m t)").bitcast(I32), y_c[g][:, cols])
 
-        def store_scales(g):
-            for q in range(4):
-                queue = nc.scalar if g == 1 and q >= 2 else nc.sync
-                queue.dma_start(
-                    out_2[g, 4 * q : 4 * q + 4, :].bitcast(I32), y_s[g][32 * q : 32 * q + 4, :].bitcast(I32)
-                )
-
         for s in range(4):
-            minus_one(s)
             block_results(s)
-        prep_w3(1, 1)
+        minus_one(6)
+        minus_one(7)
         for s in range(4, 8):
             block_results(s)
         way_up(0, 0, 512, "scalar", 0)
         way_up(0, 512, 512, "scalar", 8)
-        store_scales(0)
-        way_up(1, 0, 512, "scalar", 48)
+        store_words(0, 0, S, nc.sync)
+        way_up(1, 0, 512, "scalar", 32)
+        store_words(1, 0, 512, nc.sync)
         way_up(1, 512, 256, "scalar", 56)
         way_up(1, 768, 256, "vector", 60)
-        store_scales(1)
+        store_words(1, 512, 512, nc.sync)
+        for q in range(4):
+            queue = nc.sync if q < 2 else nc.scalar
+            queue.dma_start(
+                out_2[:, 4 * q : 4 * q + 4, :].bitcast(I32), y_s[32 * q : 32 * q + 8, :].bitcast(I32)
+            )

@@ -18,9 +18,19 @@ P = 128
 PACK = 4
 GROUP = P * PACK
 BANK = 512
+SLICES = H // P
+PER_COLUMN = 16
 SPARE = 16
 KIB = 1024
 FLOPS = 2 * (2 * K * H * S + H * H * NBLK)
+
+TABLE_PLACE = (0, 16)
+W1_PLACE = {(0, 0): 32, (1, 0): 40, (0, 1): 48, (1, 1): 56}
+W3_PLACE = {(0, 0): 16, (1, 0): 24, (0, 1): 40, (1, 1): 48}
+GV_PLACE, GH_PLACE, TABLE_SCALES_PLACE = 16, 40, 54
+PIECES = ((0, 0, 512, 0), (0, 512, 512, 8), (1, 0, 512, 32), (1, 512, 256, 56), (1, 768, 256, 60))
+FIRST_GAIN_ON_VECTOR = 5
+RUN = 64
 
 
 def tile_list_stutter_block_encoder_kernel(
@@ -40,90 +50,82 @@ def tile_list_stutter_block_encoder_kernel(
             return tile
 
         def load_table_pass(a):
-            tile = shared.tile([P, T], I32, name="tab%d" % a, offset=16 * a * KIB)
+            tile = shared.tile([P, T], I32, name="tab%d" % a, offset=TABLE_PLACE[a] * KIB)
             nc.sync.dma_start(tile[:], tab_words[a].rearrange("p t i -> p (t i)").bitcast(I32))
             return tile
 
-        def load_weight_chunk(w, a, b, raw):
-            nc.sync.dma_start(
-                raw, w[a * GROUP : (a + 1) * GROUP, b * GROUP : (b + 1) * GROUP].rearrange("(p j) c -> p j c", j=PACK)
-            )
+        def load_weight(w, a, b, name, place):
+            raw = shared.tile([P, PACK, GROUP], F32, name=name, offset=place * KIB)
+            rows = w[a * GROUP : (a + 1) * GROUP, b * GROUP : (b + 1) * GROUP]
+            nc.sync.dma_start(raw[:], rows.rearrange("(p j) c -> p j c", j=PACK))
+            return raw
 
         def load_gain(src, name, place):
-            tile = shared.tile([P, 2 * PACK], F32, name=name, offset=place * KIB)
+            tile = shared.tile([P, SLICES], F32, name=name, offset=place * KIB)
             nc.scalar.dma_start(
                 tile[:].rearrange("p (b t) -> p b t", t=PACK), src.rearrange("(b p t) -> p b t", b=2, t=PACK)
             )
             return tile
 
-        def copy_on(engine, out, in_):
-            if engine == "scalar":
-                nc.scalar.copy(out, in_)
-            else:
-                nc.vector.tensor_copy(out, in_)
+        def rounded_tile(name):
+            return ring.tile([P, PACK * BANK], BF16, name=name, tag="rounded", bufs=4, align_bytes=64)
 
-        def bf_tile(name):
-            return ring.tile([P, PACK * BANK], BF16, name=name, tag="bf", bufs=4, align_bytes=64)
+        def round_weight(raw, name):
+            rounded = rounded_tile(name)
+            dst = rounded[:].rearrange("p (t m j) -> p m j t", t=PACK, j=PACK)
+            src = raw[:].rearrange("p j (m t) -> p m j t", t=PACK)
+            for lo in range(0, P, RUN):
+                nc.scalar.copy(dst[:, lo : lo + RUN], src[:, lo : lo + RUN])
+            return rounded
 
-        def round_weight(raw, name, shares=(("scalar", 0, 64), ("scalar", 64, 128))):
-            grouped = bf_tile(name)
-            dst = grouped[:].rearrange("p (t m j) -> p m j t", t=PACK, j=PACK)
-            src = raw.rearrange("p j (m t) -> p m j t", t=PACK)
-            for engine, lo, hi in shares:
-                copy_on(engine, dst[:, lo:hi], src[:, lo:hi])
-            return grouped
+        def round_slices(four, width, name, copy):
+            rounded = rounded_tile(name)
+            dst = rounded[:, : PACK * width].rearrange("p (c i t) -> p c t i", i=PACK, t=PACK)
+            src = four.rearrange("p t (c i) -> p c t i", i=PACK)
+            for lo in range(0, width // PACK, RUN):
+                copy(dst[:, lo : lo + RUN], src[:, lo : lo + RUN])
+            return rounded
 
-        def round_rows(rows, width, name, engine):
-            grouped = bf_tile(name)
-            dst = grouped[:, : PACK * width].rearrange("p (c i t) -> p c t i", i=PACK, t=PACK)
-            src = rows.rearrange("p t (c i) -> p c t i", i=PACK)
-            for lo in range(0, width // PACK, 64):
-                copy_on(engine, dst[:, lo : lo + 64], src[:, lo : lo + 64])
-            return grouped
-
-        def quantise(grouped, name):
+        def quantise(rounded, name):
             codes = keep.tile([P, BANK], I32, name=name + "_c", align_bytes=64)
             scales = keep.tile([P, BANK], U8, name=name + "_s", align_bytes=64)
-            nc.vector.quantize_mx(out=codes[:].bitcast(FP8X4), scales=scales[:], in_=grouped[:])
+            nc.vector.quantize_mx(out=codes[:].bitcast(FP8X4), scales=scales[:], in_=rounded[:])
             return codes, scales
 
-        tab_sc = shared.tile([P, T], U8, name="tab_sc", offset=54 * KIB)
+        tab_sc = shared.tile([P, T], U8, name="tab_sc", offset=TABLE_SCALES_PLACE * KIB)
         nc.vector.memset(tab_sc[:, : T // 2].bitcast(I32), 0)
         nc.gpsimd.memset(tab_sc[:, T // 2 :].bitcast(I32), 0)
         w2_sc = keep.tile([P, 2 * H], U8, name="w2_sc", align_bytes=64)
         nc.vector.memset(w2_sc[:].bitcast(I32), 0)
         v_sc1 = keep.tile([P, S], U8, name="v_sc1", align_bytes=64)
         nc.vector.memset(v_sc1[:].bitcast(I32), 0)
-        blk = [keep.tile([P, NBLK + SPARE], F32, name="blk%d" % s, align_bytes=64) for s in range(8)]
-        for s in range(8):
+        blk = [keep.tile([P, NBLK + SPARE], F32, name="blk%d" % s, align_bytes=64) for s in range(SLICES)]
+        for s in range(SLICES):
             nc.vector.memset(blk[s][:, NBLK:], 0.0)
 
-        w1_raw = {}
-
-        def load_w1(a, b):
-            w1_raw[a, b] = shared.tile(
-                [P, PACK, BANK], F32, name="w1r%d%d" % (a, b), offset=(32 + 16 * b + 8 * a) * KIB
-            )
-            load_weight_chunk(w1, a, b, w1_raw[a, b][:])
-
-        gh_sb = load_gain(gh, "gh_sb", 40)
-        gv_sb = load_gain(gv, "gv_sb", 16)
-        neg_gh = keep.tile([P, 2 * PACK], F32, name="neg_gh")
+        gh_sb = load_gain(gh, "gh_sb", GH_PLACE)
+        gv_sb = load_gain(gv, "gv_sb", GV_PLACE)
+        neg_gh = keep.tile([P, SLICES], F32, name="neg_gh")
         nc.scalar.activation(neg_gh[:], gh_sb[:], ACT.Copy, scale=-1.0)
-        gv_wide = [keep.tile([P, NBLK], F32, name="gv_wide%d" % s, align_bytes=64) for s in range(8)]
-        for s in range(8):
+        gv_wide = [keep.tile([P, NBLK], F32, name="gv_wide%d" % s, align_bytes=64) for s in range(SLICES)]
+        for s in range(SLICES):
             nc.scalar.copy(gv_wide[s][:], gv_sb[:, s : s + 1].to_broadcast([P, NBLK]))
         tab0 = load_table_pass(0)
         offs_sb = load_list(offs, "offs_sb")
         pos1_sb = load_list(pos1, "pos1_sb")
         pos2_sb = load_list(pos2, "pos2_sb")
         pos3_sb = load_list(pos3, "pos3_sb")
+        w1_raw = {}
+
+        def load_w1(a, b):
+            w1_raw[a, b] = load_weight(w1, a, b, "w1r%d%d" % (a, b), W1_PLACE[a, b])
+
         load_w1(0, 0)
         for q in range(4):
             nc.gpsimd.dma_start(
                 tab_sc[32 * q : 32 * q + 8, :].bitcast(I32), tab_scales[:, 4 * q : 4 * q + 4, :].bitcast(I32)
             )
-        w2_raw = ring.tile([P, 4 * H], U8, name="w2_raw", tag="zf1", bufs=1, align_bytes=64)
+        w2_raw = ring.tile([P, 4 * H], U8, name="w2_raw", tag="z1", bufs=1, align_bytes=64)
         nc.sync.dma_start(
             w2_raw[:].bitcast(I32).rearrange("p (a c) -> p a c", a=2),
             w2_words.bitcast(I32).rearrange("a p c -> p a c"),
@@ -147,7 +149,7 @@ def tile_list_stutter_block_encoder_kernel(
 
         w2_c, w2_s = {}, {}
 
-        def deal_w2(b):
+        def order_w2(b):
             w2_c[b] = keep.tile([P, 2 * H], U8, name="w2_c%d" % b, align_bytes=64)
             w2_s[b] = keep.tile([P, H], U8, name="w2_s%d" % b, align_bytes=64)
             nc.vector.tensor_copy(
@@ -159,62 +161,56 @@ def tile_list_stutter_block_encoder_kernel(
                 w2_sc[:].rearrange("p (a b m t) -> p b a t m", a=2, b=2, t=PACK)[:, b],
             )
 
-        deal_w2(0)
-        w1_q, w3_q = {}, {}
+        w1_q, w3_q, z_q = {}, {}, {}
 
-        def prep_w1(a, b):
-            w1_q[a, b] = quantise(round_weight(w1_raw[a, b][:], "w1g%d%d" % (a, b)), "w1q%d%d" % (a, b))
+        def quantise_w1(a, b):
+            w1_q[a, b] = quantise(round_weight(w1_raw[a, b], "w1g%d%d" % (a, b)), "w1q%d%d" % (a, b))
 
-        prep_w1(0, 0)
-        deal_w2(1)
-        prep_w1(1, 0)
+        order_w2(0)
+        quantise_w1(0, 0)
+        order_w2(1)
+        quantise_w1(1, 0)
         for h in range(2):
+            entries = slice(h * BANK // PER_COLUMN, (h + 1) * BANK // PER_COLUMN)
             nc.vector.tensor_copy(
-                v_w[1][:, h * BANK : (h + 1) * BANK],
-                tab1[:].bitcast(U32).indirect(offs_sb[:, h * 32 : (h + 1) * 32]),
+                v_w[1][:, h * BANK : (h + 1) * BANK], tab1[:].bitcast(U32).indirect(offs_sb[:, entries])
             )
 
         w3_raw = {}
         for b in range(2):
             for a in range(2):
-                w3_raw[a, b] = shared.tile(
-                    [P, PACK, BANK], F32, name="w3r%d%d" % (a, b), offset=(16 + 24 * b + 8 * a) * KIB
-                )
-                load_weight_chunk(w3, a, b, w3_raw[a, b][:])
+                w3_raw[a, b] = load_weight(w3, a, b, "w3r%d%d" % (a, b), W3_PLACE[a, b])
 
-        def prep_w3(a, b):
-            w3_q[a, b] = quantise(round_weight(w3_raw[a, b][:], "w3g%d%d" % (a, b)), "w3q%d%d" % (a, b))
+        e = [keep.tile([P, S], F32, name="e%d" % s, align_bytes=64) for s in range(SLICES)]
+        z = [ring.tile([P, PACK, NBLK], F32, name="z%d" % b, tag="z%d" % b, bufs=1, align_bytes=64) for b in range(2)]
+        bent, first, second = {}, {}, {}
 
-        e = [keep.tile([P, S], F32, name="e%d" % s, align_bytes=64) for s in range(8)]
-        zf = [ring.tile([P, PACK, NBLK], F32, name="zf%d" % b, tag="zf%d" % b, bufs=1, align_bytes=64) for b in range(2)]
-        z_q = {}
+        def work_tile(name):
+            return ring.tile([P, BANK], F32, name=name, tag="work", bufs=8, align_bytes=64)
 
-        bent = {}
-
-        def bend(s, halves=(0, 1)):
+        def bend(s, h):
             b, t = divmod(s, PACK)
             cols = slice(t * P, (t + 1) * P)
-            for h in halves:
-                js = slice(h * BANK, (h + 1) * BANK)
-                bent_in = psum.tile([P, BANK], F32, name="bent_in", tag="pa")
-                for a in range(2):
-                    codes, scales = w1_q[a, b]
-                    nc.tensor.matmul_mx(
-                        out=bent_in[:],
-                        lhsT=codes[:, cols].bitcast(FP8X4),
-                        lhsT_scale=scales[:, cols],
-                        rhs=v_w[a][:, js].bitcast(FP8X4),
-                        rhs_scale=v_sc[a][:, js],
-                        start=(a == 0),
-                        stop=(a == 1),
-                    )
-                bent[s, h] = ring.tile([P, BANK], F32, name="bent", tag="bent", bufs=8, align_bytes=64)
-                nc.scalar.activation(bent[s, h][:], bent_in[:], ACT.Tanh)
+            js = slice(h * BANK, (h + 1) * BANK)
+            product = psum.tile([P, BANK], F32, name="product", tag="fp8")
+            for a in range(2):
+                codes, scales = w1_q[a, b]
+                nc.tensor.matmul_mx(
+                    out=product[:],
+                    lhsT=codes[:, cols].bitcast(FP8X4),
+                    lhsT_scale=scales[:, cols],
+                    rhs=v_w[a][:, js].bitcast(FP8X4),
+                    rhs_scale=v_sc[a][:, js],
+                    start=(a == 0),
+                    stop=(a == 1),
+                )
+            bent[s, h] = work_tile("bent")
+            nc.scalar.activation(bent[s, h][:], product[:], ACT.Tanh)
 
         def features(s, h):
             b, t = divmod(s, PACK)
             js = slice(h * BANK, (h + 1) * BANK)
-            linear = psum.tile([P, BANK], F32, name="linear", tag="pb")
+            linear = psum.tile([P, BANK], F32, name="linear", tag="fp4")
             for a in range(2):
                 c0 = a * GROUP + t * P
                 nc.tensor.matmul_mx(
@@ -228,110 +224,76 @@ def tile_list_stutter_block_encoder_kernel(
                 )
             nc.vector.tensor_tensor(e[s][:, js], linear[:], bent[s, h][:], ALU.add)
 
-        first, second = {}, {}
-
-        def spent(s, h, name):
-            if s < 8:
-                return bent[s, h]
-            return ring.tile([P, BANK], F32, name=name, tag="bent", bufs=8, align_bytes=64)
-
-        def first_member(s):
-            first[s] = spent(s + 1, 1, "first")
-            nc.vector.tensor_tensor(first[s][:], e[s][:].indirect(pos1_sb[:]), gv_wide[s][:], ALU.mult)
+        def first_member(s, dst):
+            first[s] = dst
+            nc.vector.tensor_tensor(dst, e[s][:].indirect(pos1_sb[:]), gv_wide[s][:], ALU.mult)
 
         def second_member(s):
-            second[s] = spent(s + 2, 0, "second")
-            nc.vector.tensor_tensor(second[s][:], e[s][:].indirect(pos2_sb[:]), first[s][:], ALU.subtract)
+            second[s] = bent[s + 2, 0] if s + 2 < SLICES else work_tile("second")
+            nc.vector.tensor_tensor(second[s][:], e[s][:].indirect(pos2_sb[:]), first[s], ALU.subtract)
 
         def gain(s):
             b, t = divmod(s, PACK)
-            if s == 7:
-                nc.vector.tensor_scalar(zf[b][:, t, :], second[s][:], neg_gh[:, s : s + 1], None, ALU.mult)
-            elif s < 6:
-                nc.gpsimd.tensor_scalar(
-                    zf[b][:, t, :], second[s][:], neg_gh[:, s : s + 1], 0.0, ALU.mult, ALU.add
-                )
+            if s >= FIRST_GAIN_ON_VECTOR:
+                nc.vector.tensor_scalar(z[b][:, t, :], second[s][:], neg_gh[:, s : s + 1], None, ALU.mult)
             else:
-                nc.scalar.activation(zf[b][:, t, :], second[s][:], ACT.Copy, scale=neg_gh[:, s : s + 1])
-
-        em = {}
+                nc.gpsimd.tensor_scalar(z[b][:, t, :], second[s][:], neg_gh[:, s : s + 1], 0.0, ALU.mult, ALU.add)
 
         def minus_one(s):
             nc.scalar.activation(e[s][:], e[s][:], ACT.Copy, bias=-1.0)
-            em[s] = e[s][:]
 
         for h in range(2):
-            bend(0, (h,))
+            bend(0, h)
             features(0, h)
-        bend(1)
-        w3_late = []
-        for s in range(7):
-            if s + 2 < 8:
-                bend(s + 2)
-            features(s + 1, 0)
-            features(s + 1, 1)
+        for h in range(2):
+            bend(1, h)
+        w3_waiting = []
+        for s in range(SLICES - 1):
+            if s + 2 < SLICES:
+                for h in range(2):
+                    bend(s + 2, h)
+            for h in range(2):
+                features(s + 1, h)
             if s > 0:
                 second_member(s - 1)
-            first_member(s)
+            first_member(s, bent[s + 1, 1][:])
             if s > 0:
                 gain(s - 1)
-            if s < 2:
-                prep_w1(s, 1)
-            elif s < 4:
-                prep_w3(s - 2, 0)
-            elif s < 6:
-                w3_late.append(round_weight(w3_raw[s - 4, 1][:], "w3g%d1" % (s - 4)))
-            if s == 4:
-                minus_one(0)
-            if s == 5:
-                zg0 = round_rows(zf[0][:], NBLK, "zg0", "scalar")
-                z_q[0] = quantise(zg0, "zq0")
-                minus_one(1)
-            if s == 6:
-                for r in range(2, 6):
-                    minus_one(r)
-        first[7] = zg0[:].bitcast(F32)[:, :NBLK]
-        nc.vector.tensor_tensor(first[7], e[7][:].indirect(pos1_sb[:]), gv_wide[7][:], ALU.mult)
-        second_member(6)
-        gain(6)
-        last = spent(9, 0, "second")
-        zg1 = bf_tile("zg1")
-        z_q[1] = (
-            keep.tile([P, BANK], I32, name="zq1_c", align_bytes=64),
-            keep.tile([P, BANK], U8, name="zq1_s", align_bytes=64),
-        )
-        halves = [slice(0, 256), slice(256, 512)]
-        for h in range(2):
-            nc.vector.tensor_tensor(
-                last[:, halves[h]], e[7][:].indirect(pos2_sb[:, 16 * h : 16 * h + 16]), first[7][:, halves[h]],
-                ALU.subtract,
-            )
-        dst = zg1[:].rearrange("p (c i t) -> p c t i", i=PACK, t=PACK)
-        src = zf[1][:].rearrange("p t (c i) -> p c t i", i=PACK)
-        nc.scalar.activation(zf[1][:, 3, halves[0]], last[:, halves[0]], ACT.Copy, scale=neg_gh[:, 7:8])
-        nc.scalar.copy(dst[:, :64], src[:, :64])
-        nc.vector.tensor_scalar(zf[1][:, 3, halves[1]], last[:, halves[1]], neg_gh[:, 7:8], None, ALU.mult)
-        nc.vector.tensor_copy(dst[:, 64:], src[:, 64:])
-        for h in (1, 0):
-            nc.vector.quantize_mx(
-                out=z_q[1][0][:, halves[h]].bitcast(FP8X4),
-                scales=z_q[1][1][:, halves[h]],
-                in_=zg1[:, 1024 * h : 1024 * h + 1024],
-            )
-        late = ring.tile([P, 2, BANK], I32, name="late", tag="zf1", bufs=1, align_bytes=64)
+            if s == PACK + 1:
+                z0_rounded = round_slices(z[0][:], NBLK, "z0_rounded", nc.scalar.copy)
+                z_q[0] = quantise(z0_rounded, "zq0")
+            b, a = divmod(s, 2)
+            if b == 0:
+                quantise_w1(a, 1)
+            elif b == 1:
+                w3_q[a, 0] = quantise(round_weight(w3_raw[a, 0], "w3g%d0" % a), "w3q%d0" % a)
+            elif b == 2:
+                w3_waiting.append(round_weight(w3_raw[a, 1], "w3g%d1" % a))
+                minus_one(a)
+            else:
+                for done in range(2, s):
+                    minus_one(done)
+        last = SLICES - 1
+        first_member(last, z0_rounded[:].bitcast(F32)[:, :NBLK])
+        second_member(last - 1)
+        second_member(last)
+        gain(last - 1)
+        gain(last)
+        z_q[1] = quantise(round_slices(z[1][:], NBLK, "z1_rounded", nc.vector.tensor_copy), "zq1")
+        w3_late = ring.tile([P, 2, BANK], I32, name="w3_late", tag="z1", bufs=1, align_bytes=64)
         for a in range(2):
             scales = keep.tile([P, BANK], U8, name="w3q%d1_s" % a, align_bytes=64)
-            nc.vector.quantize_mx(out=late[:, a, :].bitcast(FP8X4), scales=scales[:], in_=w3_late[a][:])
-            w3_q[a, 1] = (late[:, a, :], scales)
+            nc.vector.quantize_mx(out=w3_late[:, a, :].bitcast(FP8X4), scales=scales[:], in_=w3_waiting[a][:])
+            w3_q[a, 1] = (w3_late[:, a, :], scales)
 
         def block_results(s):
             b, t = divmod(s, PACK)
             cols = slice(t * P, (t + 1) * P)
-            acc = psum.tile([P, BANK], F32, name="acc", tag="pa")
+            product = psum.tile([P, BANK], F32, name="product", tag="fp8")
             for a in range(2):
                 codes, scales = w3_q[a, b]
                 nc.tensor.matmul_mx(
-                    out=acc[:],
+                    out=product[:],
                     lhsT=codes[:, cols].bitcast(FP8X4),
                     lhsT_scale=scales[:, cols],
                     rhs=z_q[a][0][:].bitcast(FP8X4),
@@ -339,47 +301,46 @@ def tile_list_stutter_block_encoder_kernel(
                     start=(a == 0),
                     stop=(a == 1),
                 )
-            nc.scalar.copy(blk[s][:, :NBLK], acc[:])
+            copy = nc.vector.tensor_copy if s == 0 else nc.scalar.copy
+            copy(blk[s][:, :NBLK], product[:])
 
         y_c = [keep.tile([P, S], I32, name="y_c%d" % g, align_bytes=64) for g in range(2)]
         y_s = keep.tile([P, S], U8, name="y_s", align_bytes=64)
 
-        def way_up(g, c0, width, engine, place):
+        def way_up(piece):
+            g, c0, width, place = piece
+            is_last = piece == PIECES[-1]
             cols = slice(c0, c0 + width)
+            entries = pos3_sb[:, c0 // PER_COLUMN : (c0 + width) // PER_COLUMN]
             y = shared.tile([P, PACK, width], F32, name="y%d_%d" % (g, c0), offset=place * KIB)
-            rows = out_0[g * GROUP : (g + 1) * GROUP, cols].rearrange("(p t) c -> p t c", t=PACK)
             for t in range(PACK):
                 s = g * PACK + t
-                nc.vector.tensor_tensor(
-                    y[:, t, :], blk[s][:].indirect(pos3_sb[:, c0 // 16 : (c0 + width) // 16]), em[s][:, cols], ALU.mult
-                )
-            queue = nc.scalar if engine == "vector" else nc.sync
-            queue.dma_start(rows, y[:])
-            grouped = round_rows(y[:], width, "yg", engine)
+                nc.vector.tensor_tensor(y[:, t, :], blk[s][:].indirect(entries), e[s][:, cols], ALU.mult)
+            queue = nc.scalar if is_last else nc.sync
+            queue.dma_start(out_0[g * GROUP : (g + 1) * GROUP, cols].rearrange("(p t) c -> p t c", t=PACK), y[:])
+            rounded = round_slices(y[:], width, "y_rounded", nc.vector.tensor_copy if is_last else nc.scalar.copy)
             nc.vector.quantize_mx(
-                out=y_c[g][:, cols].bitcast(FP8X4), scales=y_s[4 * g :, cols], in_=grouped[:, : PACK * width]
+                out=y_c[g][:, cols].bitcast(FP8X4), scales=y_s[4 * g :, cols], in_=rounded[:, : PACK * width]
             )
 
-        def store_words(g, c0, width, queue):
+        def store_words(g, c0, width):
             cols = slice(c0, c0 + width)
-            queue.dma_start(out_1[g, :, cols, :].rearrange("p m t -> p (m t)").bitcast(I32), y_c[g][:, cols])
+            nc.sync.dma_start(out_1[g, :, cols, :].rearrange("p m t -> p (m t)").bitcast(I32), y_c[g][:, cols])
 
-        for s in range(4):
+        for s in range(PACK):
             block_results(s)
-        minus_one(6)
-        minus_one(7)
-        for s in range(4, 8):
+        minus_one(last - 1)
+        minus_one(last)
+        for s in range(PACK, SLICES):
             block_results(s)
-        way_up(0, 0, 512, "scalar", 0)
-        way_up(0, 512, 512, "scalar", 8)
-        store_words(0, 0, S, nc.sync)
-        way_up(1, 0, 512, "scalar", 32)
-        store_words(1, 0, 512, nc.sync)
-        way_up(1, 512, 256, "scalar", 56)
-        way_up(1, 768, 256, "vector", 60)
-        store_words(1, 512, 512, nc.sync)
+        way_up(PIECES[0])
+        way_up(PIECES[1])
+        store_words(0, 0, S)
+        way_up(PIECES[2])
+        store_words(1, 0, S // 2)
+        way_up(PIECES[3])
+        way_up(PIECES[4])
+        store_words(1, S // 2, S // 2)
         for q in range(4):
             queue = nc.sync if q < 2 else nc.scalar
-            queue.dma_start(
-                out_2[:, 4 * q : 4 * q + 4, :].bitcast(I32), y_s[32 * q : 32 * q + 8, :].bitcast(I32)
-            )
+            queue.dma_start(out_2[:, 4 * q : 4 * q + 4, :].bitcast(I32), y_s[32 * q : 32 * q + 8, :].bitcast(I32))

from contextlib import ExitStack

import concourse.mybir as mybir

F32 = mybir.dt.float32
BF16 = mybir.dt.bfloat16
I32 = mybir.dt.int32
U32 = mybir.dt.uint32
U16 = mybir.dt.uint16
U8 = mybir.dt.uint8
FP8X4 = mybir.dt.float8_e4m3fn_x4
FP4X4 = mybir.dt.float4_e2m1fn_x4
ALU = mybir.AluOpType
ACT = mybir.ActivationFunctionType

K, H, T, S, NBLK = 1024, 1024, 4096, 1024, 512
P = 128
PACK = 4
GROUP = P * PACK
BANK = 512
SLICES = H // P
PER_COLUMN = 16
SPARE = 16
KIB = 1024
FLOPS = 2 * (2 * K * H * S + H * H * NBLK)

TABLE_PLACE = (0, 16)
W1_PLACE = {(0, 0): 32, (1, 0): 40, (0, 1): 48, (1, 1): 56}
W3_PLACE = {(0, 0): 16, (1, 0): 24, (0, 1): 40, (1, 1): 48}
GV_PLACE, GH_PLACE, TABLE_SCALES_PLACE = 16, 40, 54
PIECES = ((0, 0, 512, 0), (0, 512, 512, 8), (1, 0, 512, 32), (1, 512, 256, 56), (1, 768, 256, 60))
FIRST_GAIN_ON_VECTOR = 5
RUN = 64


def tile_list_stutter_block_encoder_kernel(
    tc, tab_words, tab_scales, offs, pos1, pos2, pos3, w1, w2_words, w2_scales, gh, gv, w3, out_0, out_1, out_2
):
    nc = tc.nc
    with ExitStack() as ctx:
        lists = ctx.enter_context(tc.tile_pool(name="lists", bufs=1))
        keep = ctx.enter_context(tc.tile_pool(name="keep", bufs=1))
        ring = ctx.enter_context(tc.tile_pool(name="ring", bufs=1))
        shared = ctx.enter_context(tc.tile_pool(name="shared", bufs=1))
        psum = ctx.enter_context(tc.psum_pool(name="psum", bufs=4))

        def load_list(src, name):
            tile = lists.tile([P, src.shape[1]], U16, name=name)
            nc.sync.dma_start(tile[:], src)
            return tile

        def load_table_pass(a):
            tile = shared.tile([P, T], I32, name="tab%d" % a, offset=TABLE_PLACE[a] * KIB)
            nc.sync.dma_start(tile[:], tab_words[a].rearrange("p t i -> p (t i)").bitcast(I32))
            return tile

        def load_weight(w, a, b, name, place):
            raw = shared.tile([P, PACK, GROUP], F32, name=name, offset=place * KIB)
            rows = w[a * GROUP : (a + 1) * GROUP, b * GROUP : (b + 1) * GROUP]
            nc.sync.dma_start(raw[:], rows.rearrange("(p j) c -> p j c", j=PACK))
            return raw

        def load_gain(src, name, place):
            tile = shared.tile([P, SLICES], F32, name=name, offset=place * KIB)
            nc.scalar.dma_start(
                tile[:].rearrange("p (b t) -> p b t", t=PACK), src.rearrange("(b p t) -> p b t", b=2, t=PACK)
            )
            return tile

        def rounded_tile(name):
            return ring.tile([P, PACK * BANK], BF16, name=name, tag="rounded", bufs=4, align_bytes=64)

        def round_weight(raw, name):
            rounded = rounded_tile(name)
            dst = rounded[:].rearrange("p (t m j) -> p m j t", t=PACK, j=PACK)
            src = raw[:].rearrange("p j (m t) -> p m j t", t=PACK)
            for lo in range(0, P, RUN):
                nc.scalar.copy(dst[:, lo : lo + RUN], src[:, lo : lo + RUN])
            return rounded

        def round_slices(four, width, name, copy):
            rounded = rounded_tile(name)
            dst = rounded[:, : PACK * width].rearrange("p (c i t) -> p c t i", i=PACK, t=PACK)
            src = four.rearrange("p t (c i) -> p c t i", i=PACK)
            for lo in range(0, width // PACK, RUN):
                copy(dst[:, lo : lo + RUN], src[:, lo : lo + RUN])
            return rounded

        def quantise(rounded, name):
            codes = keep.tile([P, BANK], I32, name=name + "_c", align_bytes=64)
            scales = keep.tile([P, BANK], U8, name=name + "_s", align_bytes=64)
            nc.vector.quantize_mx(out=codes[:].bitcast(FP8X4), scales=scales[:], in_=rounded[:])
            return codes, scales

        tab_sc = shared.tile([P, T], U8, name="tab_sc", offset=TABLE_SCALES_PLACE * KIB)
        nc.vector.memset(tab_sc[:, : T // 2].bitcast(I32), 0)
        nc.gpsimd.memset(tab_sc[:, T // 2 :].bitcast(I32), 0)
        w2_sc = keep.tile([P, 2 * H], U8, name="w2_sc", align_bytes=64)
        nc.vector.memset(w2_sc[:].bitcast(I32), 0)
        v_sc1 = keep.tile([P, S], U8, name="v_sc1", align_bytes=64)
        nc.vector.memset(v_sc1[:].bitcast(I32), 0)
        blk = [keep.tile([P, NBLK + SPARE], F32, name="blk%d" % s, align_bytes=64) for s in range(SLICES)]
        for s in range(SLICES):
            nc.vector.memset(blk[s][:, NBLK:], 0.0)

        gh_sb = load_gain(gh, "gh_sb", GH_PLACE)
        gv_sb = load_gain(gv, "gv_sb", GV_PLACE)
        neg_gh = keep.tile([P, SLICES], F32, name="neg_gh")
        nc.scalar.activation(neg_gh[:], gh_sb[:], ACT.Copy, scale=-1.0)
        gv_wide = [keep.tile([P, NBLK], F32, name="gv_wide%d" % s, align_bytes=64) for s in range(SLICES)]
        for s in range(SLICES):
            nc.scalar.copy(gv_wide[s][:], gv_sb[:, s : s + 1].to_broadcast([P, NBLK]))
        tab0 = load_table_pass(0)
        offs_sb = load_list(offs, "offs_sb")
        pos1_sb = load_list(pos1, "pos1_sb")
        pos2_sb = load_list(pos2, "pos2_sb")
        pos3_sb = load_list(pos3, "pos3_sb")
        w1_raw = {}

        def load_w1(a, b):
            w1_raw[a, b] = load_weight(w1, a, b, "w1r%d%d" % (a, b), W1_PLACE[a, b])

        load_w1(0, 0)
        for q in range(4):
            nc.gpsimd.dma_start(
                tab_sc[32 * q : 32 * q + 8, :].bitcast(I32), tab_scales[:, 4 * q : 4 * q + 4, :].bitcast(I32)
            )
        w2_raw = ring.tile([P, 4 * H], U8, name="w2_raw", tag="z1", bufs=1, align_bytes=64)
        nc.sync.dma_start(
            w2_raw[:].bitcast(I32).rearrange("p (a c) -> p a c", a=2),
            w2_words.bitcast(I32).rearrange("a p c -> p a c"),
        )
        for q in range(4):
            nc.sync.dma_start(
                w2_sc[32 * q : 32 * q + 4, :].bitcast(I32).rearrange("p (a c) -> p a c", a=2),
                w2_scales[:, 4 * q : 4 * q + 4, :].bitcast(I32).rearrange("a r c -> r a c"),
            )
        load_w1(1, 0)
        tab1 = load_table_pass(1)

        v_w = [keep.tile([P, S], U32, name="v_w%d" % a, align_bytes=64) for a in range(2)]
        v_sc0 = keep.tile([P, S], U8, name="v_sc0", align_bytes=64)
        nc.vector.tensor_copy(v_w[0][:], tab0[:].bitcast(U32).indirect(offs_sb[:]))
        nc.vector.tensor_copy(v_sc0[:], tab_sc[:].indirect(offs_sb[:]))
        nc.sync.dma_start(v_sc1[0:112, :].bitcast(I32), v_sc0[4:116, :].bitcast(I32))
        v_sc = [v_sc0, v_sc1]
        load_w1(0, 1)
        load_w1(1, 1)

        w2_c, w2_s = {}, {}

        def order_w2(b):
            w2_c[b] = keep.tile([P, 2 * H], U8, name="w2_c%d" % b, align_bytes=64)
            w2_s[b] = keep.tile([P, H], U8, name="w2_s%d" % b, align_bytes=64)
            nc.vector.tensor_copy(
                w2_c[b][:].bitcast(U16).rearrange("p (a t m) -> p a t m", a=2, t=PACK),
                w2_raw[:].bitcast(U16).rearrange("p (a b m t) -> p b a t m", a=2, b=2, t=PACK)[:, b],
            )
            nc.vector.tensor_copy(
                w2_s[b][:].rearrange("p (a t m) -> p a t m", a=2, t=PACK),
                w2_sc[:].rearrange("p (a b m t) -> p b a t m", a=2, b=2, t=PACK)[:, b],
            )

        w1_q, w3_q, z_q = {}, {}, {}

        def quantise_w1(a, b):
            w1_q[a, b] = quantise(round_weight(w1_raw[a, b], "w1g%d%d" % (a, b)), "w1q%d%d" % (a, b))

        order_w2(0)
        quantise_w1(0, 0)
        order_w2(1)
        quantise_w1(1, 0)
        for h in range(2):
            entries = slice(h * BANK // PER_COLUMN, (h + 1) * BANK // PER_COLUMN)
            nc.vector.tensor_copy(
                v_w[1][:, h * BANK : (h + 1) * BANK], tab1[:].bitcast(U32).indirect(offs_sb[:, entries])
            )

        w3_raw = {}
        for b in range(2):
            for a in range(2):
                w3_raw[a, b] = load_weight(w3, a, b, "w3r%d%d" % (a, b), W3_PLACE[a, b])

        e = [keep.tile([P, S], F32, name="e%d" % s, align_bytes=64) for s in range(SLICES)]
        z = [ring.tile([P, PACK, NBLK], F32, name="z%d" % b, tag="z%d" % b, bufs=1, align_bytes=64) for b in range(2)]
        bent, first, second = {}, {}, {}

        def work_tile(name):
            return ring.tile([P, BANK], F32, name=name, tag="work", bufs=8, align_bytes=64)

        def bend(s, h):
            b, t = divmod(s, PACK)
            cols = slice(t * P, (t + 1) * P)
            js = slice(h * BANK, (h + 1) * BANK)
            product = psum.tile([P, BANK], F32, name="product", tag="fp8")
            for a in range(2):
                codes, scales = w1_q[a, b]
                nc.tensor.matmul_mx(
                    out=product[:],
                    lhsT=codes[:, cols].bitcast(FP8X4),
                    lhsT_scale=scales[:, cols],
                    rhs=v_w[a][:, js].bitcast(FP8X4),
                    rhs_scale=v_sc[a][:, js],
                    start=(a == 0),
                    stop=(a == 1),
                )
            bent[s, h] = work_tile("bent")
            nc.scalar.activation(bent[s, h][:], product[:], ACT.Tanh)

        def features(s, h):
            b, t = divmod(s, PACK)
            js = slice(h * BANK, (h + 1) * BANK)
            linear = psum.tile([P, BANK], F32, name="linear", tag="fp4")
            for a in range(2):
                c0 = a * GROUP + t * P
                nc.tensor.matmul_mx(
                    out=linear[:],
                    lhsT=w2_c[b][:, 2 * c0 : 2 * (c0 + P)].bitcast(FP4X4),
                    lhsT_scale=w2_s[b][:, c0 : c0 + P],
                    rhs=v_w[a][:, js].bitcast(FP8X4),
                    rhs_scale=v_sc[a][:, js],
                    start=(a == 0),
                    stop=(a == 1),
                )
            nc.vector.tensor_tensor(e[s][:, js], linear[:], bent[s, h][:], ALU.add)

        def first_member(s, dst):
            first[s] = dst
            nc.vector.tensor_tensor(dst, e[s][:].indirect(pos1_sb[:]), gv_wide[s][:], ALU.mult)

        def second_member(s):
            second[s] = bent[s + 2, 0] if s + 2 < SLICES else work_tile("second")
            nc.vector.tensor_tensor(second[s][:], e[s][:].indirect(pos2_sb[:]), first[s], ALU.subtract)

        def gain(s):
            b, t = divmod(s, PACK)
            if s >= FIRST_GAIN_ON_VECTOR:
                nc.vector.tensor_scalar(z[b][:, t, :], second[s][:], neg_gh[:, s : s + 1], None, ALU.mult)
            else:
                nc.gpsimd.tensor_scalar(z[b][:, t, :], second[s][:], neg_gh[:, s : s + 1], 0.0, ALU.mult, ALU.add)

        def minus_one(s):
            nc.scalar.activation(e[s][:], e[s][:], ACT.Copy, bias=-1.0)

        for h in range(2):
            bend(0, h)
            features(0, h)
        for h in range(2):
            bend(1, h)
        w3_waiting = []
        for s in range(SLICES - 1):
            if s + 2 < SLICES:
                for h in range(2):
                    bend(s + 2, h)
            for h in range(2):
                features(s + 1, h)
            if s > 0:
                second_member(s - 1)
            first_member(s, bent[s + 1, 1][:])
            if s > 0:
                gain(s - 1)
            if s == PACK + 1:
                z0_rounded = round_slices(z[0][:], NBLK, "z0_rounded", nc.scalar.copy)
                z_q[0] = quantise(z0_rounded, "zq0")
            b, a = divmod(s, 2)
            if b == 0:
                quantise_w1(a, 1)
            elif b == 1:
                w3_q[a, 0] = quantise(round_weight(w3_raw[a, 0], "w3g%d0" % a), "w3q%d0" % a)
            elif b == 2:
                w3_waiting.append(round_weight(w3_raw[a, 1], "w3g%d1" % a))
                minus_one(a)
            else:
                for done in range(2, s):
                    minus_one(done)
        last = SLICES - 1
        first_member(last, z0_rounded[:].bitcast(F32)[:, :NBLK])
        second_member(last - 1)
        second_member(last)
        gain(last - 1)
        gain(last)
        z_q[1] = quantise(round_slices(z[1][:], NBLK, "z1_rounded", nc.vector.tensor_copy), "zq1")
        w3_late = ring.tile([P, 2, BANK], I32, name="w3_late", tag="z1", bufs=1, align_bytes=64)
        for a in range(2):
            scales = keep.tile([P, BANK], U8, name="w3q%d1_s" % a, align_bytes=64)
            nc.vector.quantize_mx(out=w3_late[:, a, :].bitcast(FP8X4), scales=scales[:], in_=w3_waiting[a][:])
            w3_q[a, 1] = (w3_late[:, a, :], scales)

        def block_results(s):
            b, t = divmod(s, PACK)
            cols = slice(t * P, (t + 1) * P)
            product = psum.tile([P, BANK], F32, name="product", tag="fp8")
            for a in range(2):
                codes, scales = w3_q[a, b]
                nc.tensor.matmul_mx(
                    out=product[:],
                    lhsT=codes[:, cols].bitcast(FP8X4),
                    lhsT_scale=scales[:, cols],
                    rhs=z_q[a][0][:].bitcast(FP8X4),
                    rhs_scale=z_q[a][1][:],
                    start=(a == 0),
                    stop=(a == 1),
                )
            copy = nc.vector.tensor_copy if s == 0 else nc.scalar.copy
            copy(blk[s][:, :NBLK], product[:])

        y_c = [keep.tile([P, S], I32, name="y_c%d" % g, align_bytes=64) for g in range(2)]
        y_s = keep.tile([P, S], U8, name="y_s", align_bytes=64)

        def way_up(piece):
            g, c0, width, place = piece
            is_last = piece == PIECES[-1]
            cols = slice(c0, c0 + width)
            entries = pos3_sb[:, c0 // PER_COLUMN : (c0 + width) // PER_COLUMN]
            y = shared.tile([P, PACK, width], F32, name="y%d_%d" % (g, c0), offset=place * KIB)
            for t in range(PACK):
                s = g * PACK + t
                nc.vector.tensor_tensor(y[:, t, :], blk[s][:].indirect(entries), e[s][:, cols], ALU.mult)
            queue = nc.scalar if is_last else nc.sync
            queue.dma_start(out_0[g * GROUP : (g + 1) * GROUP, cols].rearrange("(p t) c -> p t c", t=PACK), y[:])
            rounded = round_slices(y[:], width, "y_rounded", nc.vector.tensor_copy if is_last else nc.scalar.copy)
            nc.vector.quantize_mx(
                out=y_c[g][:, cols].bitcast(FP8X4), scales=y_s[4 * g :, cols], in_=rounded[:, : PACK * width]
            )

        def store_words(g, c0, width):
            cols = slice(c0, c0 + width)
            nc.sync.dma_start(out_1[g, :, cols, :].rearrange("p m t -> p (m t)").bitcast(I32), y_c[g][:, cols])

        for s in range(PACK):
            block_results(s)
        minus_one(last - 1)
        minus_one(last)
        for s in range(PACK, SLICES):
            block_results(s)
        way_up(PIECES[0])
        way_up(PIECES[1])
        store_words(0, 0, S)
        way_up(PIECES[2])
        store_words(1, 0, S // 2)
        way_up(PIECES[3])
        way_up(PIECES[4])
        store_words(1, S // 2, S // 2)
        for q in range(4):
            queue = nc.sync if q < 2 else nc.scalar
            queue.dma_start(out_2[:, 4 * q : 4 * q + 4, :].bitcast(I32), y_s[32 * q : 32 * q + 8, :].bitcast(I32))
